import numpy as np, ml_dtypes
CORES = [2,3,42,43,82,83,122,123]
N = 8
BF = ml_dtypes.bfloat16
def gentries(a):
    return np.ascontiguousarray(a.reshape(8, 16, -1).transpose(0, 2, 1)).reshape(8, -1)
def gtable(e):
    e = np.asarray(e); return np.ascontiguousarray(e.reshape(8, -1, 16).transpose(0, 2, 1)).reshape(128, -1).astype(np.int32)
H, E, L = 4096, 64, 2
M = (N - 1) * E
def slot(r, q):
    return q - (1 if q > r else 0)
def flat(a):
    return np.ascontiguousarray(np.asarray(a).astype(np.int64).transpose(1, 0, 2)).reshape(8, -1)
def perms(rng):
    return np.argsort(rng.random((N, 8, H)), axis=-1)
def mesh(c, w, lens):
    nx, pv, tw = np.empty((N, 8, H), np.int64), np.empty((N, 8, H), np.int64), np.empty((N, 8, H), np.int64)
    for r in range(N):
        for g in range(8):
            e = np.add.accumulate(lens[r, g]); e = np.append(e[e < H], H); s = np.append(0, e[:-1])
            k = np.arange(1, H + 1); k[e - 1] = s; a = w[r, g]
            nx[r, g, a] = H * r + a[k]; pv[r, g, a[k]] = H * r + a
            b = c[r, g, M:].reshape(-1, 2); tw[r, g, b] = H * r + b[:, ::-1]
            for q in range(N):
                if q != r:
                    i, j = E * slot(r, q), E * slot(q, r)
                    tw[r, g, c[r, g, i:i + E]] = H * q + c[q, g, j:j + E]
    return {"nxt": nx.astype(np.int32), "prv": pv.astype(np.int32), "twn": tw.astype(np.int32), "far": np.stack([gtable(c[r, :, :M]) for r in range(N)])}
def draw(v, c, w, lens):
    d = {"x": v.astype(np.float32).astype(BF)}; d.update(mesh(c, w, lens)); return d
def setup_inputs(rng):
    v = rng.integers(-31, 32, (N, 128, H))
    return draw(v, perms(rng), perms(rng), rng.integers(3, 9, (N, 8, H)))
def setup_inputs_long(rng):
    v = rng.integers(-31, 32, (N, 128, H)); k = (np.arange(N)[:, None] + np.arange(8) + rng.integers(0, 3)) % 3
    lens = rng.integers(1, 3, (N, 8, H)); lens[k == 0] = H
    lens = np.where((k == 2)[:, :, None], rng.integers(1, 201, (N, 8, H)), lens)
    return draw(v, perms(rng), perms(rng), lens)
def setup_inputs_near(rng):
    v = np.where(rng.random((N, 128, H)) < 0.875, 31, -31); a = np.arange(H)
    e = np.append(a[:M // 2], a[H - M // 2:]); mid = a[M // 2:H - M // 2]; c = np.empty((N, 8, H), np.int64); c[:, :, M:] = mid
    for r in range(N):
        for g in range(8): c[r, g, :M] = rng.permutation(e)
    w = np.broadcast_to(a, (N, 8, H))
    return draw(v, c, w, rng.integers(2, 6, (N, 8, H)))
def setup_inputs_hops(rng):
    v = rng.integers(-31, 32, (N, 128, H)); c = perms(rng); w = c.copy()
    for r in range(N):
        for g in range(4): w[r, g, :M] = rng.permutation(c[r, g, :M])
    return draw(v, c, w, rng.integers(3, 17, (N, 8, H)))
def setup_inputs_spread(rng):
    v = (rng.integers(-31, 32, (N, 128, H)) >> rng.integers(0, 5, (N, 1, H))) * (rng.random((N, 1, H)) > 0.0625)
    return draw(v, perms(rng), perms(rng), 2 ** rng.integers(0, 8, (N, 8, H)))
def check_inputs(d):
    bad = []
    try:
        v = np.asarray(d["x"]).astype(np.float32)
        if not (v.shape == (N, 128, H) and np.isfinite(v).all() and (np.abs(v) <= 31).all() and (v == np.floor(v)).all()): bad.append("x: whole numbers from -31 to 31")
        nx, pv, tw = [np.asarray(d[k]).astype(np.int64) for k in ("nxt", "prv", "twn")]
        own = np.broadcast_to(np.arange(N)[:, None, None], (N, 8, H))
        if not all(a.shape == (N, 8, H) and (a >= 0).all() and (a < N * H).all() for a in (nx, pv, tw)): return bad + ["nxt, prv, twn: range"]
        if not ((nx // H == own).all() and (pv // H == own).all()): bad.append("nxt, prv: same rank")
        n, p, t = flat(nx), flat(pv), flat(tw); me = np.arange(N * H)
        if any((p[g][n[g]] != me).any() or (n[g][p[g]] != me).any() for g in range(8)): bad.append("nxt and prv: one undoes the other")
        if any((t[g][t[g]] != me).any() or (t[g] == me).any() for g in range(8)): bad.append("twn: pairs")
        for r in range(N):
            for q in range(N):
                if q != r and (np.sum(tw[r] // H == q, axis=1) != E).any(): bad.append("twn: E far twins a pair")
        f = np.stack([gentries(np.asarray(a).astype(np.int64)) for a in d["far"]])
        if not (f.shape == (N, 8, M) and (f >= 0).all() and (f < H).all()): return bad + ["far: range"]
        u = np.sort(f, axis=-1)
        if (u[..., 1:] == u[..., :-1]).any(): bad.append("far: all different")
        for r in range(N):
            for q in range(N):
                if q != r:
                    i, j = E * slot(r, q), E * slot(q, r)
                    if any((tw[r, g][f[r, g, i:i + E]] != H * q + f[q, g, j:j + E]).any() for g in range(8)): bad.append("far: order")
    except Exception:
        bad.append("shapes")
    return bad
def reference(x, nxt, prv, twn, far):
    v = x.astype(np.float32).reshape(N, 8, 16, H).transpose(1, 2, 0, 3).reshape(8, 16, N * H)
    n, p, t = flat(nxt), flat(prv), flat(twn)
    for k in range(L):
        W = v.shape[2]; v2 = np.empty((8, 16, 2 * W), np.float32); n2, p2 = np.empty((8, 2 * W), np.int64), np.empty((8, 2 * W), np.int64)
        for g in range(8):
            m = v[g] + v[g][:, n[g]]
            v2[g, :, 0::2] = m; v2[g, :, 1::2] = m[:, n[g]]
            n2[g, 0::2] = 2 * n[g]; n2[g, 1::2] = 2 * p[g][t[g]] + 1
            p2[g, 0::2] = 2 * p[g]; p2[g, 1::2] = 2 * t[g][n[g]] + 1
        v, n, p = v2, n2, p2; t = np.broadcast_to(np.arange(2 * W) ^ 1, (8, 2 * W))
    y = v.reshape(8, 16, N, -1)[..., 1::2].transpose(2, 0, 1, 3)
    return {"y": np.ascontiguousarray(y).reshape(N, 128, -1).astype(BF), "nx": np.ascontiguousarray(n.reshape(8, N, -1).transpose(1, 0, 2)).astype(np.float32)}

@@ -1,0 +1,288 @@
+from concourse.bass import DstId, RemoteDMATransfer
+from concourse.mybir import dt, AluOpType, ActivationFunctionType
+
+H, E, NS = 4096, 64, 7
+M = NS * E
+HX = H + M
+BFD, F32, I32, U16 = "bfloat16", "float32", "int32", "uint16"
+SCRATCH = {"NX": ("sbuf", [128, 1024], F32), "EQ": ("sbuf", [128, 16, 16], BFD), "BM": ("sbuf", [128, 24], F32),
+           "Y": ("sbuf", [128, 2 * H], BFD), "FA": ("sbuf", [128, 28], I32), "SI": ("sbuf", [128, 64], F32)}
+for _k in ("X", "X2", "M2", "U2", "N1", "N3", "NN", "NT", "Q"):
+    SCRATCH[_k] = ("sbuf", [128, H], BFD)
+for _k in ("N2", "MX", "UX"):
+    SCRATCH[_k] = ("sbuf", [128, HX], BFD)
+for _k in ("NA", "PA", "TA"):
+    SCRATCH[_k] = ("sbuf", [128, 256], I32)
+for _k in ("NH", "NL", "PH", "PL", "TH", "TL", "TNH", "TNL", "PTH", "PTL"):
+    SCRATCH[_k] = ("sbuf", [128, 256], BFD)
+for _k in ("TMP", "TMP2"):
+    SCRATCH[_k] = ("sbuf", [128, 256], F32)
+for _k in ("D0", "D1", "D2"):
+    SCRATCH[_k] = ("sbuf", [128, 16, 128], BFD)
+for _k in ("LI", "LA"):
+    SCRATCH[_k] = ("sbuf", [128, 8], I32)
+for _k in ("LM", "HI", "OF", "BB"):
+    SCRATCH[_k] = ("sbuf", [128, 16], F32)
+for _k in ("C2", "C3", "R1", "XF", "MF", "EE", "VV"):
+    SCRATCH[_k] = ("sbuf", [128, M], BFD)
+for _k in ("FW", "NFW", "PFW", "EW"):
+    SCRATCH[_k] = ("sbuf", [128, 32], U16)
+for _k in ("NXW", "TWL", "PTW"):
+    SCRATCH[_k] = ("sbuf", [128, 256], U16)
+for _k in range(8):
+    SCRATCH["ps%d" % _k] = ("psum", [128, 512], F32)
+SEMAPHORES = ["vec", "act", "ten", "gps", "ldn", "ldp", "ldt", "ldf", "xa", "xb", "xc", "xd", "m2a", "m2b", "u2a", "u2b",
+              "lan1", "lan3", "lan2", "otn", "opt", "stn", "sty", "a1", "an", "a2", "s1", "sn", "s2"]
+ADD, SUB, MUL = AluOpType.add, AluOpType.subtract, AluOpType.mult
+IDN = ActivationFunctionType.Identity
+
+
+def slot(r, q):
+    return q - (1 if q > r else 0)
+
+
+def rank_program(g, core, T, topo):
+    r = T.rank_of(core)
+    if r is None:
+        return
+    base = H * r
+    cores = T.cores
+    total, seen = {}, {}
+
+    def inc(op, s, n=1):
+        op.then_inc(T.sem[s], n)
+        total[s] = total.get(s, 0) + n
+        return (s, total[s])
+
+    def wait(qn, q, toks):
+        best = {}
+        for s, v in toks:
+            best[s] = max(best.get(s, 0), v)
+        for s in best:
+            if seen.get((qn, s), 0) < best[s]:
+                q.wait_ge(T.sem[s], best[s])
+                seen[(qn, s)] = best[s]
+
+    V, S, P, Y = g.vector, g.scalar, g.tensor, g.sync
+
+    def vec(f, *toks):
+        wait("v", V, toks)
+        return inc(f(), "vec")
+
+    def act(f, *toks):
+        wait("s", S, toks)
+        return inc(f(), "act")
+
+    def gps(f, *toks):
+        wait("g", g, toks)
+        return inc(f(), "gps")
+
+    def sdma(sem, out, in_, *toks):
+        wait("y", Y, toks)
+        return inc(Y.dma_start(out, in_), sem, 16)
+
+    def wrap(ps, n, d, src, c0, *toks):
+        wait("t", P, toks)
+        tok = None
+        for p in range(16):
+            mm = P.matmul(ps[:, 0:n], d[:, p, :], src[:, 16 * c0 + p:16 * (c0 + n):16], p == 0, p == 15)
+            if p == 15:
+                tok = inc(mm, "ten")
+        return tok
+
+    def evac(out, ps, n, *toks):
+        return vec(lambda: V.tensor_scalar(out, ps[:, 0:n], float(base), None, SUB), *toks)
+
+    def lane(t, k, w=H):
+        return t[k:128:16, 0:w]
+
+    ldn = sdma("ldn", T.NA[:, :], T.nxt[:, :])
+    ldp = sdma("ldp", T.PA[:, :], T.prv[:, :])
+    ldf = inc(S.dma_start(T.FA[:, :], T.far[:, :]), "ldf", 16)
+    ldt = inc(S.dma_start(T.TA[:, :], T.twn[:, :]), "ldt", 16)
+    xa = sdma("xa", T.X[:, 0:2048], T.x[:, 0:2048])
+
+    v_eq = vec(lambda: V.memset(T.EQ[:, :, :], 1.0))
+    v_bm = vec(lambda: V.memset(T.BM[:, :], 1.0))
+    v_n1 = vec(lambda: V.memset(T.N1[:, :], 0.0))
+    GE, IE = AluOpType.is_ge, AluOpType.is_equal
+    g_eq = gps(lambda: g.affine_select(T.EQ[:, :, :], T.EQ[:, :, :], [[1, 16], [-1, 16]], IE, 0.0, 0, 0), v_eq)
+    g_b1 = gps(lambda: g.affine_select(T.BM[:, :], T.BM[:, :], [[-2, 3], [-16, 8]], GE, 0.0, 0, 1), v_bm)
+    g_bm = gps(lambda: g.affine_select(T.BM[:, :], T.BM[:, :], [[2, 3], [16, 8]], GE, 0.0, 1, -1), g_b1)
+    g_li = gps(lambda: g.iota(T.LI[:, 0:1], [[0, 1]], 0, 1))
+
+    def iot(ap, pat, b):
+        return gps(lambda: g.iota(ap, pat, b, 0, allow_small_or_imprecise_dtypes=True))
+    if r > 0:
+        iot(T.HI[:, 0:r], [[H, r]], H + 256 * ((r - 1) // 4))
+        iot(T.OF[:, 0:r], [[0, r]], 64 * ((r - 1) % 4))
+    if r < NS:
+        iot(T.HI[:, r:NS], [[H, NS - r]], H * (r + 2) + 256 * (r // 4))
+        iot(T.OF[:, r:NS], [[0, NS - r]], 64 * (r % 4))
+    iot(T.HI[:, 7:8], [[0, 1]], 0)
+    iot(T.OF[:, 7:8], [[0, 1]], 0)
+    iot(T.HI[:, 8:16], [[256, 2], [0, 4]], base + H)
+    iot(T.OF[:, 8:16], [[0, 2], [64, 4]], 0)
+    g_si = iot(T.SI[:, :], [[1, 64]], 0)
+    g_n2 = iot(T.N2[:, 0:2048], [[0, 2048]], 0)
+
+    v_la = vec(lambda: V.tensor_scalar(T.LA[:, 0:1], T.LI[:, 0:1], 15, None, AluOpType.bitwise_and), g_li)
+    v_l2 = vec(lambda: V.tensor_scalar(T.LM[:, 0:1], T.LA[:, 0:1], 2.0, None, IE), v_la)
+    v_l3 = vec(lambda: V.tensor_scalar(T.LM[:, 4:5], T.LA[:, 0:1], 3.0, None, IE), v_la)
+    v_h = vec(lambda: V.tensor_scalar(T.HI[:, :], T.HI[:, :], T.LM[:, 0:1], None, MUL), v_l2, g_si)
+    v_o = vec(lambda: V.tensor_scalar(T.OF[:, :], T.OF[:, :], T.LM[:, 4:5], None, MUL), v_l3, g_si)
+    v_bb = vec(lambda: V.tensor_tensor(T.BB[:, :], T.HI[:, :], T.OF[:, :], ADD), v_h, v_o)
+
+    def build(u):
+        tok = None
+        d = T["D%d" % u]
+        for k in range(8):
+            tok = act(lambda: S.activation(d[:, :, 16 * k:16 * k + 16], T.EQ[:, :, :], IDN,
+                                           scale=T.BM[:, 8 * u + k:8 * u + k + 1]), g_eq, g_bm)
+        return tok
+
+    def codes(c, o):
+        tok = None
+        for i in range(NS):
+            tok = act(lambda: S.activation(c[:, E * i:E * i + E], T.SI[:, :], IDN, bias=T.BB[:, o + i:o + i + 1],
+                                           scale=T.LM[:, 4:5]), v_bb, g_si)
+        return tok
+
+    def split(a, h, l, ld):
+        t = vec(lambda: V.tensor_copy(h[:, :], a[:, :]), ld)
+        return vec(lambda: V.tensor_tensor(l[:, :], a[:, :], h[:, :], SUB), t)
+    v_nl = split(T.NA, T.NH, T.NL, ldn)
+    v_pl = split(T.PA, T.PH, T.PL, ldp)
+    v_fw = vec(lambda: V.tensor_copy(T.FW[:, 0:28], T.FA[:, :]), ldf)
+    v_tl = split(T.TA, T.TH, T.TL, ldt)
+    v_n3 = vec(lambda: V.memset(T.N3[:, :], 0.0))
+    v_n2 = vec(lambda: V.memset(T.N2[:, 2048:H], 0.0))
+
+    sdma("lan1", lane(T.N1, 0), T.NH[:, :], v_n1, v_nl)
+    sdma("lan1", lane(T.N1, 1), T.NL[:, :])
+    sdma("lan1", lane(T.N1, 4), T.PH[:, :], v_pl)
+    lan1 = sdma("lan1", lane(T.N1, 5), T.PL[:, :])
+    xb = sdma("xb", T.X[:, 2048:H], T.x[:, 2048:H])
+    sdma("lan3", lane(T.N3, 2), T.TH[:, :], v_n3, v_tl)
+    lan3 = sdma("lan3", lane(T.N3, 3), T.TL[:, :])
+    xc = sdma("xc", T.X2[:, 0:2048], T.x[:, 0:2048])
+    sdma("lan2", lane(T.N2, 6), T.TH[:, :], v_n2, g_n2)
+    sdma("lan2", lane(T.N2, 7), T.TL[:, :])
+    for k in (2, 4):
+        sdma("lan2", lane(T.N2, k), T.PH[:, :])
+        lan2 = sdma("lan2", lane(T.N2, k + 1), T.PL[:, :])
+    xd = sdma("xd", T.X2[:, 2048:H], T.x[:, 2048:H])
+
+    s_d0 = build(0)
+    s_c2 = codes(T.C2, 0)
+    s_d2 = build(2)
+    s_xf = act(lambda: S.activation(T.XF[:, :], T.X[:, :].indirect(T.FW[:, 0:28]), IDN), v_fw, xa, xb)
+    s_c3 = codes(T.C3, 8)
+    s_d1 = build(1)
+
+    v_r1 = vec(lambda: V.tensor_tensor(T.R1[:, :], T.N1[:, :].indirect(T.FW[:, 0:28]), T.C2[:, :], ADD), lan1, s_c2, v_fw)
+    t_nf = wrap(T.ps0, 28, T.D0, T.R1, 0, v_r1, s_d0)
+    t_na = wrap(T.ps2, 128, T.D0, T.N1, 0, lan1)
+    t_pf = wrap(T.ps1, 28, T.D2, T.R1, 0, s_d2)
+    t_nb = wrap(T.ps3, 128, T.D0, T.N1, 128)
+    v_x0 = vec(lambda: V.tensor_scalar(T.NX[:, 0:1024:4], T.NA[:, :], 4.0, None, MUL))
+    v_nf = evac(T.NFW[:, 0:28], T.ps0, 28, t_nf)
+    v_mf = vec(lambda: V.tensor_tensor(T.MF[:, :], T.X[:, :].indirect(T.NFW[:, 0:28]), T.XF[:, :], ADD), v_nf, s_xf, xa, xb)
+    v_c3 = vec(lambda: V.tensor_copy(T.N3[:, :].indirect(T.FW[:, 0:28]), T.C3[:, :]), lan3, s_c3)
+    v_na = evac(T.NXW[:, 0:128], T.ps2, 128, t_na)
+
+    def m_pass(a, b, *toks):
+        return vec(lambda: V.tensor_tensor(T.MX[:, 16 * a:16 * b], T.X[:, :].indirect(T.NXW[:, a:b]), T.X2[:, 16 * a:16 * b],
+                                           ADD), xa, xb, *toks)
+    v_ma = m_pass(0, 128, v_na, xc)
+    m2a = sdma("m2a", T.M2[:, 0:2048], T.MX[:, 0:2048], v_ma)
+    v_pf = evac(T.PFW[:, 0:28], T.ps1, 28, t_pf)
+    v_ee = vec(lambda: V.tensor_copy(T.EE[:, :], T.N3[:, :].indirect(T.PFW[:, 0:28])), v_pf, v_c3)
+    v_nb = evac(T.NXW[:, 128:256], T.ps3, 128, t_nb)
+    t_ta = wrap(T.ps4, 128, T.D1, T.N3, 0, v_c3, s_d1)
+    t_e = wrap(T.ps6, 28, T.D1, T.EE, 0, v_ee)
+    t_tb = wrap(T.ps5, 128, T.D1, T.N3, 128)
+    v_mb = m_pass(128, 192, v_nb, xd)
+    v_ta = evac(T.TWL[:, 0:128], T.ps4, 128, t_ta)
+    v_mc = m_pass(192, 256, v_nb, xd)
+    m2b = sdma("m2b", T.M2[:, 2048:H], T.MX[:, 2048:H], v_mc)
+    v_e = evac(T.EW[:, 0:28], T.ps6, 28, t_e)
+
+    def order():
+        used, plan = [], []
+        away = [q for q in range(8) if q != r and topo.chip(cores[q]) != topo.chip(core)]
+        near = [q for q in range(8) if q != r and topo.chip(cores[q]) == topo.chip(core)]
+        for q in away + near:
+            es = topo.engines(core, cores[q])
+            es = es[::2] + es[1::2]
+            e = [k for k in es if k not in used][0]
+            used.append(e)
+            plan.append((q, e))
+        return plan
+    plan = order()
+
+    def send(src, dst, rs, ls, *toks):
+        wait("g", g, toks)
+        tr = []
+        for q, e in plan:
+            rid, pid, _se = topo.addr(cores[q])
+            i, k = slot(r, q), slot(q, r)
+            tr.append(RemoteDMATransfer(dst_ids=[DstId(rid=rid, pnc=pid)], dma_engine_mask=1 << e, remote_sem=T.sem[rs],
+                                        src=src[:, E * i:E * i + E], dst=dst[:, H + E * k:H + E * k + E]))
+        g.remote_dma_fused(tr, local_sem=T.sem[ls])
+        total[ls] = NS
+        total[rs] = NS
+    a1, an, a2 = ("a1", NS), ("an", NS), ("a2", NS)
+    send(T.MF, T.MX, "a1", "s1", v_mf)
+    send(T.R1, T.N2, "an", "sn", v_r1)
+
+    v_vv = vec(lambda: V.tensor_copy(T.VV[:, :], T.MX[:, :].indirect(T.EW[:, 0:28])), a1, v_ma, v_mb, v_mc, v_e)
+    send(T.VV, T.UX, "a2", "s2", v_vv)
+
+    s_nn = None
+    for h, tk in ((0, v_na), (1, v_nb)):
+        s_nn = act(lambda: S.activation(T.NN[:, 2048 * h:2048 * h + 2048],
+                                        T.N2[:, 0:H].indirect(T.NXW[:, 128 * h:128 * h + 128]), IDN), lan2, tk)
+    v_tb = evac(T.TWL[:, 128:256], T.ps5, 128, t_tb)
+    v_q = []
+    for h, tk in ((0, m2a), (1, m2b)):
+        v_q.append(vec(lambda: V.tensor_tensor(T.Q[:, 2048 * h:2048 * h + 2048],
+                                               T.MX[:, 0:H].indirect(T.NXW[:, 128 * h:128 * h + 128]),
+                                               T.M2[:, 2048 * h:2048 * h + 2048], ADD), v_mc, v_nb, tk))
+    s_nt = []
+    for h, tk in ((0, v_ta), (1, v_tb)):
+        s_nt.append(act(lambda: S.activation(T.NT[:, 2048 * h:2048 * h + 2048],
+                                             T.N2[:, :].indirect(T.TWL[:, 128 * h:128 * h + 128]), IDN), lan2, an, tk))
+    t_pa = wrap(T.ps7, 128, T.D1, T.NT, 0, s_nt[0])
+    t_pb = wrap(T.ps0, 128, T.D1, T.NT, 128, s_nt[1], v_nf)
+    v_ua = vec(lambda: V.tensor_copy(T.UX[:, 0:2048], T.MX[:, :].indirect(T.TWL[:, 0:128])), a1, v_ta)
+    s_ub = act(lambda: S.activation(T.UX[:, 2048:H], T.MX[:, :].indirect(T.TWL[:, 128:256]), IDN), a1, v_mc, v_tb)
+
+    sdma("otn", T.TNH[:, :], lane(T.NN, 6), s_nn)
+    otn = sdma("otn", T.TNL[:, :], lane(T.NN, 7))
+    u2a = sdma("u2a", T.U2[:, 0:2048], T.UX[:, 0:2048], v_ua)
+    sdma("opt", T.PTH[:, :], lane(T.NT, 4), s_nt[1])
+    opt = sdma("opt", T.PTL[:, :], lane(T.NT, 5))
+    u2b = sdma("u2b", T.U2[:, 2048:H], T.UX[:, 2048:H], s_ub)
+    v_t1 = vec(lambda: V.tensor_tensor(T.TMP[:, :], T.TNH[:, :], T.TNL[:, :], ADD), otn)
+    v_x3 = vec(lambda: V.tensor_scalar(T.NX[:, 3:1024:4], T.PA[:, :], 4.0, 1.0, MUL, ADD))
+    v_x1 = vec(lambda: V.tensor_scalar(T.NX[:, 1:1024:4], T.TMP[:, :], 4.0, 3.0, MUL, ADD), v_t1)
+    v_pa = evac(T.PTW[:, 0:128], T.ps7, 128, t_pa)
+    v_pb = evac(T.PTW[:, 128:256], T.ps0, 128, t_pb)
+
+    s_ye, v_yo = [], []
+    for k in range(4):
+        s_ye.append(act(lambda: S.activation(T.Y[:, 2048 * k:2048 * k + 2048:2],
+                                             T.Q[:, :].indirect(T.NXW[:, 64 * k:64 * k + 64]), IDN), v_q[0], v_q[1]))
+    for k in range(4):
+        v_yo.append(vec(lambda: V.tensor_tensor(T.Y[:, 2048 * k + 1:2048 * k + 2048:2],
+                                                T.UX[:, :].indirect(T.PTW[:, 64 * k:64 * k + 64]),
+                                                T.U2[:, 1024 * k:1024 * k + 1024], ADD), a2, v_ua, s_ub, v_pa, v_pb,
+                        u2a if k < 2 else u2b))
+        sdma("sty", T.y[:, 2048 * k:2048 * k + 2048], T.Y[:, 2048 * k:2048 * k + 2048], s_ye[k], v_yo[k])
+        if k == 1:
+            v_t2 = vec(lambda: V.tensor_tensor(T.TMP2[:, :], T.PTH[:, :], T.PTL[:, :], ADD), opt)
+            v_x2 = vec(lambda: V.tensor_scalar(T.NX[:, 2:1024:4], T.TMP2[:, :], 4.0, 2.0, MUL, ADD), v_t2)
+            sdma("stn", T.nx[:, :], T.NX[:, :], v_x0, v_x1, v_x2, v_x3)
+
+    wait("g", g, [(s, total[s]) for s in total])

@@ -5,11 +5,11 @@ H, E, NS = 4096, 64, 7
 M = NS * E
 HX = H + M
 BFD, F32, I32, U16 = "bfloat16", "float32", "int32", "uint16"
-SCRATCH = {"NX": ("sbuf", [128, 1024], F32), "EQ": ("sbuf", [128, 16, 16], BFD), "BM": ("sbuf", [128, 24], F32),
+SCRATCH = {"NX": ("sbuf", [128, 1024], F32), "EQ": ("sbuf", [128, 16, 16], BFD), "BM": ("sbuf", [128, 16], F32),
            "Y": ("sbuf", [128, 2 * H], BFD), "FA": ("sbuf", [128, 28], I32), "SI": ("sbuf", [128, 64], F32)}
-for _k in ("X", "X2", "M2", "U2", "N1", "N3", "NN", "NT", "Q"):
+for _k in ("X", "X2", "M2", "U2", "N3", "NN", "NT", "Q"):
     SCRATCH[_k] = ("sbuf", [128, H], BFD)
-for _k in ("N2", "MX", "UX"):
+for _k in ("NW", "MX", "UX"):
     SCRATCH[_k] = ("sbuf", [128, HX], BFD)
 for _k in ("NA", "PA", "TA"):
     SCRATCH[_k] = ("sbuf", [128, 256], I32)
@@ -17,13 +17,13 @@ for _k in ("NH", "NL", "PH", "PL", "TH", "TL", "TNH", "TNL", "PTH", "PTL"):
     SCRATCH[_k] = ("sbuf", [128, 256], BFD)
 for _k in ("TMP", "TMP2"):
     SCRATCH[_k] = ("sbuf", [128, 256], F32)
-for _k in ("D0", "D1", "D2"):
+for _k in ("D0", "D1"):
     SCRATCH[_k] = ("sbuf", [128, 16, 128], BFD)
 for _k in ("LI", "LA"):
     SCRATCH[_k] = ("sbuf", [128, 8], I32)
 for _k in ("LM", "HI", "OF", "BB"):
-    SCRATCH[_k] = ("sbuf", [128, 16], F32)
-for _k in ("C2", "C3", "R1", "XF", "MF", "EE", "VV"):
+    SCRATCH[_k] = ("sbuf", [128, 8], F32)
+for _k in ("C3", "R1", "RN", "XF", "MF", "EE", "VV"):
     SCRATCH[_k] = ("sbuf", [128, M], BFD)
 for _k in ("FW", "NFW", "PFW", "EW"):
     SCRATCH[_k] = ("sbuf", [128, 32], U16)
@@ -31,10 +31,11 @@ for _k in ("NXW", "TWL", "PTW"):
     SCRATCH[_k] = ("sbuf", [128, 256], U16)
 for _k in range(8):
     SCRATCH["ps%d" % _k] = ("psum", [128, 512], F32)
-SEMAPHORES = ["vec", "act", "ten", "gps", "ldn", "ldp", "ldt", "ldf", "xa", "xb", "xc", "xd", "m2a", "m2b", "u2a", "u2b",
-              "lan1", "lan3", "lan2", "otn", "opt", "stn", "sty", "a1", "an", "a2", "s1", "sn", "s2"]
+SEMAPHORES = ["vec", "act", "ten", "gps", "ldn", "ldp", "ldt", "ldf", "xa", "xb", "xc", "xd", "m2a", "m2b", "u20", "u21", "u22",
+              "u23", "lan1", "lan3", "rnl", "otn", "opt", "stn", "sty", "a1", "an", "a2", "s1", "sn", "s2"]
 ADD, SUB, MUL = AluOpType.add, AluOpType.subtract, AluOpType.mult
 IDN = ActivationFunctionType.Identity
+CHUNKS = [(0, 64), (64, 128), (128, 192), (192, 224), (224, 240), (240, 256)]
 
 
 def slot(r, q):
@@ -81,57 +82,78 @@ def rank_program(g, core, T, topo):
         wait("y", Y, toks)
         return inc(Y.dma_start(out, in_), sem, 16)
 
-    def wrap(ps, n, d, src, c0, *toks):
+    def wrap(b, n, d, src, c0, *toks):
         wait("t", P, toks)
         tok = None
         for p in range(16):
-            mm = P.matmul(ps[:, 0:n], d[:, p, :], src[:, 16 * c0 + p:16 * (c0 + n):16], p == 0, p == 15)
+            mm = P.matmul(T["ps%d" % b][:, 0:n], d[:, p, :], src[:, 16 * c0 + p:16 * (c0 + n):16], p == 0, p == 15)
             if p == 15:
                 tok = inc(mm, "ten")
         return tok
 
-    def evac(out, ps, n, *toks):
-        return vec(lambda: V.tensor_scalar(out, ps[:, 0:n], float(base), None, SUB), *toks)
+    def evac(out, b, n, tok):
+        return vec(lambda: V.tensor_scalar(out, T["ps%d" % b][:, 0:n], float(base), None, SUB), tok)
 
-    def lane(t, k, w=H):
-        return t[k:128:16, 0:w]
+    def lane(t, k):
+        return t[k:128:16, 0:H]
+
+    def qd(t, k):
+        return t[:, 64 * k:64 * k + 64]
+
+    def rows(t, k):
+        return t[:, 1024 * k:1024 * k + 1024]
 
     ldn = sdma("ldn", T.NA[:, :], T.nxt[:, :])
     ldp = sdma("ldp", T.PA[:, :], T.prv[:, :])
     ldf = inc(S.dma_start(T.FA[:, :], T.far[:, :]), "ldf", 16)
     ldt = inc(S.dma_start(T.TA[:, :], T.twn[:, :]), "ldt", 16)
     xa = sdma("xa", T.X[:, 0:2048], T.x[:, 0:2048])
+    xb = sdma("xb", T.X[:, 2048:H], T.x[:, 2048:H])
 
     v_eq = vec(lambda: V.memset(T.EQ[:, :, :], 1.0))
     v_bm = vec(lambda: V.memset(T.BM[:, :], 1.0))
-    v_n1 = vec(lambda: V.memset(T.N1[:, :], 0.0))
+    v_nw = vec(lambda: V.memset(T.NW[:, 0:H], 0.0))
     GE, IE = AluOpType.is_ge, AluOpType.is_equal
     g_eq = gps(lambda: g.affine_select(T.EQ[:, :, :], T.EQ[:, :, :], [[1, 16], [-1, 16]], IE, 0.0, 0, 0), v_eq)
-    g_b1 = gps(lambda: g.affine_select(T.BM[:, :], T.BM[:, :], [[-2, 3], [-16, 8]], GE, 0.0, 0, 1), v_bm)
-    g_bm = gps(lambda: g.affine_select(T.BM[:, :], T.BM[:, :], [[2, 3], [16, 8]], GE, 0.0, 1, -1), g_b1)
+    g_b1 = gps(lambda: g.affine_select(T.BM[:, :], T.BM[:, :], [[-2, 2], [-16, 8]], GE, 0.0, 0, 1), v_bm)
+    g_bm = gps(lambda: g.affine_select(T.BM[:, :], T.BM[:, :], [[2, 2], [16, 8]], GE, 0.0, 1, -1), g_b1)
     g_li = gps(lambda: g.iota(T.LI[:, 0:1], [[0, 1]], 0, 1))
 
     def iot(ap, pat, b):
         return gps(lambda: g.iota(ap, pat, b, 0, allow_small_or_imprecise_dtypes=True))
-    if r > 0:
-        iot(T.HI[:, 0:r], [[H, r]], H + 256 * ((r - 1) // 4))
-        iot(T.OF[:, 0:r], [[0, r]], 64 * ((r - 1) % 4))
-    if r < NS:
-        iot(T.HI[:, r:NS], [[H, NS - r]], H * (r + 2) + 256 * (r // 4))
-        iot(T.OF[:, r:NS], [[0, NS - r]], 64 * (r % 4))
-    iot(T.HI[:, 7:8], [[0, 1]], 0)
-    iot(T.OF[:, 7:8], [[0, 1]], 0)
-    iot(T.HI[:, 8:16], [[256, 2], [0, 4]], base + H)
-    iot(T.OF[:, 8:16], [[0, 2], [64, 4]], 0)
+    iot(T.HI[:, :], [[256, 2], [0, 4]], base + H)
+    iot(T.OF[:, :], [[0, 2], [64, 4]], 0)
     g_si = iot(T.SI[:, :], [[1, 64]], 0)
-    g_n2 = iot(T.N2[:, 0:2048], [[0, 2048]], 0)
+    g_n3 = iot(T.N3[:, 0:2048], [[0, 2048]], 0)
 
+    def split(a, h, l, ld):
+        t = vec(lambda: V.tensor_copy(h[:, :], a[:, :]), ld)
+        return vec(lambda: V.tensor_tensor(l[:, :], a[:, :], h[:, :], SUB), t)
+    v_nl = split(T.NA, T.NH, T.NL, ldn)
+    v_pl = split(T.PA, T.PH, T.PL, ldp)
+    v_tl = split(T.TA, T.TH, T.TL, ldt)
+    v_fw = vec(lambda: V.tensor_copy(T.FW[:, 0:28], T.FA[:, :]), ldf)
     v_la = vec(lambda: V.tensor_scalar(T.LA[:, 0:1], T.LI[:, 0:1], 15, None, AluOpType.bitwise_and), g_li)
     v_l2 = vec(lambda: V.tensor_scalar(T.LM[:, 0:1], T.LA[:, 0:1], 2.0, None, IE), v_la)
     v_l3 = vec(lambda: V.tensor_scalar(T.LM[:, 4:5], T.LA[:, 0:1], 3.0, None, IE), v_la)
     v_h = vec(lambda: V.tensor_scalar(T.HI[:, :], T.HI[:, :], T.LM[:, 0:1], None, MUL), v_l2, g_si)
     v_o = vec(lambda: V.tensor_scalar(T.OF[:, :], T.OF[:, :], T.LM[:, 4:5], None, MUL), v_l3, g_si)
     v_bb = vec(lambda: V.tensor_tensor(T.BB[:, :], T.HI[:, :], T.OF[:, :], ADD), v_h, v_o)
+    v_n3 = vec(lambda: V.memset(T.N3[:, 2048:H], 0.0))
+    v_x0 = vec(lambda: V.tensor_scalar(T.NX[:, 0:1024:4], T.NA[:, :], 4.0, None, MUL), ldn)
+    v_x3 = vec(lambda: V.tensor_scalar(T.NX[:, 3:1024:4], T.PA[:, :], 4.0, 1.0, MUL, ADD), ldp)
+
+    sdma("lan1", lane(T.NW, 0), T.NH[:, :], v_nw, v_nl)
+    sdma("lan1", lane(T.NW, 1), T.NL[:, :])
+    for k in (2, 4):
+        sdma("lan1", lane(T.NW, k), T.PH[:, :], v_pl)
+        sdma("lan1", lane(T.NW, k + 1), T.PL[:, :])
+    sdma("lan1", lane(T.NW, 6), T.TH[:, :], v_tl)
+    lan1 = sdma("lan1", lane(T.NW, 7), T.TL[:, :])
+    sdma("lan3", lane(T.N3, 2), T.TH[:, :], v_n3, g_n3)
+    lan3 = sdma("lan3", lane(T.N3, 3), T.TL[:, :])
+    xc = sdma("xc", T.X2[:, 0:2048], T.x[:, 0:2048])
+    xd = sdma("xd", T.X2[:, 2048:H], T.x[:, 2048:H])
 
     def build(u):
         tok = None
@@ -140,73 +162,34 @@ def rank_program(g, core, T, topo):
             tok = act(lambda: S.activation(d[:, :, 16 * k:16 * k + 16], T.EQ[:, :, :], IDN,
                                            scale=T.BM[:, 8 * u + k:8 * u + k + 1]), g_eq, g_bm)
         return tok
-
-    def codes(c, o):
-        tok = None
-        for i in range(NS):
-            tok = act(lambda: S.activation(c[:, E * i:E * i + E], T.SI[:, :], IDN, bias=T.BB[:, o + i:o + i + 1],
-                                           scale=T.LM[:, 4:5]), v_bb, g_si)
-        return tok
-
-    def split(a, h, l, ld):
-        t = vec(lambda: V.tensor_copy(h[:, :], a[:, :]), ld)
-        return vec(lambda: V.tensor_tensor(l[:, :], a[:, :], h[:, :], SUB), t)
-    v_nl = split(T.NA, T.NH, T.NL, ldn)
-    v_pl = split(T.PA, T.PH, T.PL, ldp)
-    v_fw = vec(lambda: V.tensor_copy(T.FW[:, 0:28], T.FA[:, :]), ldf)
-    v_tl = split(T.TA, T.TH, T.TL, ldt)
-    v_n3 = vec(lambda: V.memset(T.N3[:, :], 0.0))
-    v_n2 = vec(lambda: V.memset(T.N2[:, 2048:H], 0.0))
-
-    sdma("lan1", lane(T.N1, 0), T.NH[:, :], v_n1, v_nl)
-    sdma("lan1", lane(T.N1, 1), T.NL[:, :])
-    sdma("lan1", lane(T.N1, 4), T.PH[:, :], v_pl)
-    lan1 = sdma("lan1", lane(T.N1, 5), T.PL[:, :])
-    xb = sdma("xb", T.X[:, 2048:H], T.x[:, 2048:H])
-    sdma("lan3", lane(T.N3, 2), T.TH[:, :], v_n3, v_tl)
-    lan3 = sdma("lan3", lane(T.N3, 3), T.TL[:, :])
-    xc = sdma("xc", T.X2[:, 0:2048], T.x[:, 0:2048])
-    sdma("lan2", lane(T.N2, 6), T.TH[:, :], v_n2, g_n2)
-    sdma("lan2", lane(T.N2, 7), T.TL[:, :])
-    for k in (2, 4):
-        sdma("lan2", lane(T.N2, k), T.PH[:, :])
-        lan2 = sdma("lan2", lane(T.N2, k + 1), T.PL[:, :])
-    xd = sdma("xd", T.X2[:, 2048:H], T.x[:, 2048:H])
-
     s_d0 = build(0)
-    s_c2 = codes(T.C2, 0)
-    s_d2 = build(2)
-    s_xf = act(lambda: S.activation(T.XF[:, :], T.X[:, :].indirect(T.FW[:, 0:28]), IDN), v_fw, xa, xb)
-    s_c3 = codes(T.C3, 8)
     s_d1 = build(1)
+    s_xf = act(lambda: S.activation(T.XF[:, :], T.X[:, :].indirect(T.FW[:, 0:28]), IDN), v_fw, xa, xb)
+    s_c3 = None
+    for i in range(NS):
+        s_c3 = act(lambda: S.activation(T.C3[:, E * i:E * i + E], T.SI[:, :], IDN, bias=T.BB[:, i:i + 1],
+                                        scale=T.LM[:, 4:5]), v_bb, g_si)
+    s_ce = act(lambda: S.activation(T.NW[:, H:HX], T.C3[:, :], IDN), s_c3)
 
-    v_r1 = vec(lambda: V.tensor_tensor(T.R1[:, :], T.N1[:, :].indirect(T.FW[:, 0:28]), T.C2[:, :], ADD), lan1, s_c2, v_fw)
-    t_nf = wrap(T.ps0, 28, T.D0, T.R1, 0, v_r1, s_d0)
-    t_na = wrap(T.ps2, 128, T.D0, T.N1, 0, lan1)
-    t_pf = wrap(T.ps1, 28, T.D2, T.R1, 0, s_d2)
-    t_nb = wrap(T.ps3, 128, T.D0, T.N1, 128)
-    v_x0 = vec(lambda: V.tensor_scalar(T.NX[:, 0:1024:4], T.NA[:, :], 4.0, None, MUL))
-    v_nf = evac(T.NFW[:, 0:28], T.ps0, 28, t_nf)
+    v_r1 = vec(lambda: V.tensor_copy(T.R1[:, :], T.NW[:, 0:H].indirect(T.FW[:, 0:28])), lan1, v_fw)
+    t_nq = [wrap(0, 64, T.D0, T.NW, 0, lan1, s_d0)]
+    t_nf = wrap(1, 28, T.D0, T.R1, 0, v_r1)
+    t_nq += [wrap(3, 64, T.D0, T.NW, 64), wrap(4, 64, T.D0, T.NW, 128)]
+    t_pf = wrap(2, 28, T.D1, T.R1, 0, s_d1)
+    t_nq.append(wrap(5, 64, T.D0, T.NW, 192))
+    v_nq = [evac(qd(T.NXW, 0), 0, 64, t_nq[0])]
+    v_nf = evac(T.NFW[:, 0:28], 1, 28, t_nf)
     v_mf = vec(lambda: V.tensor_tensor(T.MF[:, :], T.X[:, :].indirect(T.NFW[:, 0:28]), T.XF[:, :], ADD), v_nf, s_xf, xa, xb)
+    v_nq.append(evac(qd(T.NXW, 1), 3, 64, t_nq[1]))
     v_c3 = vec(lambda: V.tensor_copy(T.N3[:, :].indirect(T.FW[:, 0:28]), T.C3[:, :]), lan3, s_c3)
-    v_na = evac(T.NXW[:, 0:128], T.ps2, 128, t_na)
-
-    def m_pass(a, b, *toks):
-        return vec(lambda: V.tensor_tensor(T.MX[:, 16 * a:16 * b], T.X[:, :].indirect(T.NXW[:, a:b]), T.X2[:, 16 * a:16 * b],
-                                           ADD), xa, xb, *toks)
-    v_ma = m_pass(0, 128, v_na, xc)
-    m2a = sdma("m2a", T.M2[:, 0:2048], T.MX[:, 0:2048], v_ma)
-    v_pf = evac(T.PFW[:, 0:28], T.ps1, 28, t_pf)
+    v_nq.append(evac(qd(T.NXW, 2), 4, 64, t_nq[2]))
+    v_pf = evac(T.PFW[:, 0:28], 2, 28, t_pf)
     v_ee = vec(lambda: V.tensor_copy(T.EE[:, :], T.N3[:, :].indirect(T.PFW[:, 0:28])), v_pf, v_c3)
-    v_nb = evac(T.NXW[:, 128:256], T.ps3, 128, t_nb)
-    t_ta = wrap(T.ps4, 128, T.D1, T.N3, 0, v_c3, s_d1)
-    t_e = wrap(T.ps6, 28, T.D1, T.EE, 0, v_ee)
-    t_tb = wrap(T.ps5, 128, T.D1, T.N3, 128)
-    v_mb = m_pass(128, 192, v_nb, xd)
-    v_ta = evac(T.TWL[:, 0:128], T.ps4, 128, t_ta)
-    v_mc = m_pass(192, 256, v_nb, xd)
-    m2b = sdma("m2b", T.M2[:, 2048:H], T.MX[:, 2048:H], v_mc)
-    v_e = evac(T.EW[:, 0:28], T.ps6, 28, t_e)
+    v_nq.append(evac(qd(T.NXW, 3), 5, 64, t_nq[3]))
+    t_tw = [wrap(6, 64, T.D1, T.N3, 0, v_c3), wrap(7, 64, T.D1, T.N3, 64)]
+    t_e = wrap(1, 28, T.D1, T.EE, 0, v_ee, v_nf)
+    t_tw.append(wrap(0, 64, T.D1, T.N3, 128, v_nq[0]))
+    t_tw.append(wrap(2, 64, T.D1, T.N3, 192, v_pf))
 
     def order():
         used, plan = [], []
@@ -221,68 +204,77 @@ def rank_program(g, core, T, topo):
         return plan
     plan = order()
 
-    def send(src, dst, rs, ls, *toks):
+    def send(src, dst, d0, rs, ls, *toks):
         wait("g", g, toks)
         tr = []
         for q, e in plan:
             rid, pid, _se = topo.addr(cores[q])
             i, k = slot(r, q), slot(q, r)
             tr.append(RemoteDMATransfer(dst_ids=[DstId(rid=rid, pnc=pid)], dma_engine_mask=1 << e, remote_sem=T.sem[rs],
-                                        src=src[:, E * i:E * i + E], dst=dst[:, H + E * k:H + E * k + E]))
+                                        src=src[:, E * i:E * i + E], dst=dst[:, d0 + E * k:d0 + E * k + E]))
         g.remote_dma_fused(tr, local_sem=T.sem[ls])
         total[ls] = NS
         total[rs] = NS
     a1, an, a2 = ("a1", NS), ("an", NS), ("a2", NS)
-    send(T.MF, T.MX, "a1", "s1", v_mf)
-    send(T.R1, T.N2, "an", "sn", v_r1)
+    send(T.R1, T.RN, 0, "an", "sn", v_r1)
+    send(T.MF, T.MX, H, "a1", "s1", v_mf)
+    sdma("rnl", T.NW[4:128:16, H:HX], T.RN[4:128:16, :], an, s_ce)
+    rnl = sdma("rnl", T.NW[5:128:16, H:HX], T.RN[5:128:16, :])
 
-    v_vv = vec(lambda: V.tensor_copy(T.VV[:, :], T.MX[:, :].indirect(T.EW[:, 0:28])), a1, v_ma, v_mb, v_mc, v_e)
-    send(T.VV, T.UX, "a2", "s2", v_vv)
+    def m_pass(k):
+        return vec(lambda: V.tensor_tensor(rows(T.MX, k), T.X[:, :].indirect(qd(T.NXW, k)), rows(T.X2, k), ADD),
+                   v_nq[k], xa, xb, xc if k < 2 else xd)
+    v_m = [m_pass(0)]
+    v_tw = [evac(qd(T.TWL, 0), 6, 64, t_tw[0])]
+    v_m.append(m_pass(1))
+    m2a = sdma("m2a", T.M2[:, 0:2048], T.MX[:, 0:2048], v_m[1])
+    v_tw.append(evac(qd(T.TWL, 1), 7, 64, t_tw[1]))
+    v_m.append(m_pass(2))
+    v_e = evac(T.EW[:, 0:28], 1, 28, t_e)
+    v_tw.append(evac(qd(T.TWL, 2), 0, 64, t_tw[2]))
+    v_m.append(m_pass(3))
+    v_tw.append(evac(qd(T.TWL, 3), 2, 64, t_tw[3]))
+    m2b = sdma("m2b", T.M2[:, 2048:H], T.MX[:, 2048:H], v_m[3])
 
     s_nn = None
-    for h, tk in ((0, v_na), (1, v_nb)):
-        s_nn = act(lambda: S.activation(T.NN[:, 2048 * h:2048 * h + 2048],
-                                        T.N2[:, 0:H].indirect(T.NXW[:, 128 * h:128 * h + 128]), IDN), lan2, tk)
-    v_tb = evac(T.TWL[:, 128:256], T.ps5, 128, t_tb)
-    v_q = []
-    for h, tk in ((0, m2a), (1, m2b)):
-        v_q.append(vec(lambda: V.tensor_tensor(T.Q[:, 2048 * h:2048 * h + 2048],
-                                               T.MX[:, 0:H].indirect(T.NXW[:, 128 * h:128 * h + 128]),
-                                               T.M2[:, 2048 * h:2048 * h + 2048], ADD), v_mc, v_nb, tk))
-    s_nt = []
-    for h, tk in ((0, v_ta), (1, v_tb)):
-        s_nt.append(act(lambda: S.activation(T.NT[:, 2048 * h:2048 * h + 2048],
-                                             T.N2[:, :].indirect(T.TWL[:, 128 * h:128 * h + 128]), IDN), lan2, an, tk))
-    t_pa = wrap(T.ps7, 128, T.D1, T.NT, 0, s_nt[0])
-    t_pb = wrap(T.ps0, 128, T.D1, T.NT, 128, s_nt[1], v_nf)
-    v_ua = vec(lambda: V.tensor_copy(T.UX[:, 0:2048], T.MX[:, :].indirect(T.TWL[:, 0:128])), a1, v_ta)
-    s_ub = act(lambda: S.activation(T.UX[:, 2048:H], T.MX[:, :].indirect(T.TWL[:, 128:256]), IDN), a1, v_mc, v_tb)
+    for k in range(4):
+        s_nn = act(lambda: S.activation(rows(T.NN, k), T.NW[:, 0:H].indirect(qd(T.NXW, k)), IDN), lan1, v_nq[k])
+
+    def q_pass(h):
+        return vec(lambda: V.tensor_tensor(T.Q[:, 2048 * h:2048 * h + 2048], T.MX[:, 0:H].indirect(T.NXW[:, 128 * h:128 * h + 128]),
+                                           T.M2[:, 2048 * h:2048 * h + 2048], ADD), v_m[3], v_nq[3], (m2a, m2b)[h])
+    v_vv = vec(lambda: V.tensor_copy(T.VV[:, :], T.MX[:, :].indirect(T.EW[:, 0:28])), a1, v_m[3], v_e)
+    send(T.VV, T.UX, H, "a2", "s2", v_vv)
+    v_qa = q_pass(0)
+    v_qb = q_pass(1)
+
+    s_nt, t_pt = [], []
+    free = [v_nq[1], v_nq[2], v_nq[3], v_tw[0]]
+    for k in range(4):
+        s_nt.append(act(lambda: S.activation(rows(T.NT, k), T.NW[:, :].indirect(qd(T.TWL, k)), IDN), rnl, s_ce, v_tw[k]))
+        t_pt.append(wrap(3 + k, 64, T.D1, T.NT, 64 * k, s_nt[k], free[k]))
 
     sdma("otn", T.TNH[:, :], lane(T.NN, 6), s_nn)
     otn = sdma("otn", T.TNL[:, :], lane(T.NN, 7))
-    u2a = sdma("u2a", T.U2[:, 0:2048], T.UX[:, 0:2048], v_ua)
-    sdma("opt", T.PTH[:, :], lane(T.NT, 4), s_nt[1])
+    sdma("opt", T.PTH[:, :], lane(T.NT, 4), s_nt[3])
     opt = sdma("opt", T.PTL[:, :], lane(T.NT, 5))
-    u2b = sdma("u2b", T.U2[:, 2048:H], T.UX[:, 2048:H], s_ub)
-    v_t1 = vec(lambda: V.tensor_tensor(T.TMP[:, :], T.TNH[:, :], T.TNL[:, :], ADD), otn)
-    v_x3 = vec(lambda: V.tensor_scalar(T.NX[:, 3:1024:4], T.PA[:, :], 4.0, 1.0, MUL, ADD))
-    v_x1 = vec(lambda: V.tensor_scalar(T.NX[:, 1:1024:4], T.TMP[:, :], 4.0, 3.0, MUL, ADD), v_t1)
-    v_pa = evac(T.PTW[:, 0:128], T.ps7, 128, t_pa)
-    v_pb = evac(T.PTW[:, 128:256], T.ps0, 128, t_pb)
 
-    s_ye, v_yo = [], []
+    u, u2 = [], []
     for k in range(4):
-        s_ye.append(act(lambda: S.activation(T.Y[:, 2048 * k:2048 * k + 2048:2],
-                                             T.Q[:, :].indirect(T.NXW[:, 64 * k:64 * k + 64]), IDN), v_q[0], v_q[1]))
-    for k in range(4):
-        v_yo.append(vec(lambda: V.tensor_tensor(T.Y[:, 2048 * k + 1:2048 * k + 2048:2],
-                                                T.UX[:, :].indirect(T.PTW[:, 64 * k:64 * k + 64]),
-                                                T.U2[:, 1024 * k:1024 * k + 1024], ADD), a2, v_ua, s_ub, v_pa, v_pb,
-                        u2a if k < 2 else u2b))
-        sdma("sty", T.y[:, 2048 * k:2048 * k + 2048], T.Y[:, 2048 * k:2048 * k + 2048], s_ye[k], v_yo[k])
-        if k == 1:
-            v_t2 = vec(lambda: V.tensor_tensor(T.TMP2[:, :], T.PTH[:, :], T.PTL[:, :], ADD), opt)
-            v_x2 = vec(lambda: V.tensor_scalar(T.NX[:, 2:1024:4], T.TMP2[:, :], 4.0, 2.0, MUL, ADD), v_t2)
-            sdma("stn", T.nx[:, :], T.NX[:, :], v_x0, v_x1, v_x2, v_x3)
+        u.append(act(lambda: S.activation(rows(T.UX, k), T.MX[:, :].indirect(qd(T.TWL, k)), IDN), a1, v_m[3], v_tw[k]))
+        u2.append(sdma("u2%d" % k, rows(T.U2, k), rows(T.UX, k), u[k]))
+
+    v_t1 = vec(lambda: V.tensor_tensor(T.TMP[:, :], T.TNH[:, :], T.TNL[:, :], ADD), otn)
+    v_x1 = vec(lambda: V.tensor_scalar(T.NX[:, 1:1024:4], T.TMP[:, :], 4.0, 3.0, MUL, ADD), v_t1)
+    v_pt = [evac(qd(T.PTW, k), 3 + k, 64, t_pt[k]) for k in range(4)]
+    v_t2 = vec(lambda: V.tensor_tensor(T.TMP2[:, :], T.PTH[:, :], T.PTL[:, :], ADD), opt)
+    v_x2 = vec(lambda: V.tensor_scalar(T.NX[:, 2:1024:4], T.TMP2[:, :], 4.0, 2.0, MUL, ADD), v_t2)
+    sdma("stn", T.nx[:, :], T.NX[:, :], v_x0, v_x1, v_x2, v_x3)
+
+    for a, b in CHUNKS:
+        s_ye = act(lambda: S.activation(T.Y[:, 32 * a:32 * b:2], T.Q[:, :].indirect(T.NXW[:, a:b]), IDN), v_qa, v_qb)
+        v_yo = vec(lambda: V.tensor_tensor(T.Y[:, 32 * a + 1:32 * b:2], T.UX[:, :].indirect(T.PTW[:, a:b]), T.U2[:, 16 * a:16 * b],
+                                           ADD), a2, u2[a // 64], v_pt[a // 64], *u)
+        sdma("sty", T.y[:, 32 * a:32 * b], T.Y[:, 32 * a:32 * b], s_ye, v_yo)
 
     wait("g", g, [(s, total[s]) for s in total])

from concourse.bass import DstId, RemoteDMATransfer
from concourse.mybir import dt, AluOpType, ActivationFunctionType

H, E, NS = 4096, 64, 7
M = NS * E
HX = H + M
BFD, F32, I32, U16 = "bfloat16", "float32", "int32", "uint16"
SCRATCH = {"NX": ("sbuf", [128, 1024], F32), "EQ": ("sbuf", [128, 16, 16], BFD), "BM": ("sbuf", [128, 16], F32),
           "Y": ("sbuf", [128, 2 * H], BFD), "FA": ("sbuf", [128, 28], I32), "SI": ("sbuf", [128, 64], F32)}
for _k in ("X", "X2", "M2", "U2", "N3", "NN", "NT", "Q"):
    SCRATCH[_k] = ("sbuf", [128, H], BFD)
for _k in ("NW", "MX", "UX"):
    SCRATCH[_k] = ("sbuf", [128, HX], BFD)
for _k in ("NA", "PA", "TA"):
    SCRATCH[_k] = ("sbuf", [128, 256], I32)
for _k in ("NH", "NL", "PH", "PL", "TH", "TL", "TNH", "TNL", "PTH", "PTL"):
    SCRATCH[_k] = ("sbuf", [128, 256], BFD)
for _k in ("TMP", "TMP2"):
    SCRATCH[_k] = ("sbuf", [128, 256], F32)
for _k in ("D0", "D1"):
    SCRATCH[_k] = ("sbuf", [128, 16, 128], BFD)
for _k in ("LI", "LA"):
    SCRATCH[_k] = ("sbuf", [128, 8], I32)
for _k in ("LM", "HI", "OF", "BB"):
    SCRATCH[_k] = ("sbuf", [128, 8], F32)
for _k in ("C3", "R1", "RN", "XF", "MF", "EE", "VV"):
    SCRATCH[_k] = ("sbuf", [128, M], BFD)
for _k in ("FW", "NFW", "PFW", "EW"):
    SCRATCH[_k] = ("sbuf", [128, 32], U16)
for _k in ("NXW", "TWL", "PTW"):
    SCRATCH[_k] = ("sbuf", [128, 256], U16)
for _k in range(8):
    SCRATCH["ps%d" % _k] = ("psum", [128, 512], F32)
SEMAPHORES = ["vec", "act", "ten", "gps", "ldn", "ldp", "ldt", "ldf", "xa", "xb", "xc", "xd", "m2a", "m2b", "u20", "u21", "u22",
              "u23", "lan1", "lan3", "rnl", "otn", "opt", "stn", "sty", "a1", "an", "a2", "s1", "sn", "s2"]
ADD, SUB, MUL = AluOpType.add, AluOpType.subtract, AluOpType.mult
IDN = ActivationFunctionType.Identity
CHUNKS = [(0, 64), (64, 128), (128, 192), (192, 224), (224, 240), (240, 256)]


def slot(r, q):
    return q - (1 if q > r else 0)


def rank_program(g, core, T, topo):
    r = T.rank_of(core)
    if r is None:
        return
    base = H * r
    cores = T.cores
    total, seen = {}, {}

    def inc(op, s, n=1):
        op.then_inc(T.sem[s], n)
        total[s] = total.get(s, 0) + n
        return (s, total[s])

    def wait(qn, q, toks):
        best = {}
        for s, v in toks:
            best[s] = max(best.get(s, 0), v)
        for s in best:
            if seen.get((qn, s), 0) < best[s]:
                q.wait_ge(T.sem[s], best[s])
                seen[(qn, s)] = best[s]

    V, S, P, Y = g.vector, g.scalar, g.tensor, g.sync

    def vec(f, *toks):
        wait("v", V, toks)
        return inc(f(), "vec")

    def act(f, *toks):
        wait("s", S, toks)
        return inc(f(), "act")

    def gps(f, *toks):
        wait("g", g, toks)
        return inc(f(), "gps")

    def sdma(sem, out, in_, *toks):
        wait("y", Y, toks)
        return inc(Y.dma_start(out, in_), sem, 16)

    def wrap(b, n, d, src, c0, *toks):
        wait("t", P, toks)
        tok = None
        for p in range(16):
            mm = P.matmul(T["ps%d" % b][:, 0:n], d[:, p, :], src[:, 16 * c0 + p:16 * (c0 + n):16], p == 0, p == 15)
            if p == 15:
                tok = inc(mm, "ten")
        return tok

    def evac(out, b, n, tok):
        return vec(lambda: V.tensor_scalar(out, T["ps%d" % b][:, 0:n], float(base), None, SUB), tok)

    def lane(t, k):
        return t[k:128:16, 0:H]

    def qd(t, k):
        return t[:, 64 * k:64 * k + 64]

    def rows(t, k):
        return t[:, 1024 * k:1024 * k + 1024]

    ldn = sdma("ldn", T.NA[:, :], T.nxt[:, :])
    ldp = sdma("ldp", T.PA[:, :], T.prv[:, :])
    ldf = inc(S.dma_start(T.FA[:, :], T.far[:, :]), "ldf", 16)
    ldt = inc(S.dma_start(T.TA[:, :], T.twn[:, :]), "ldt", 16)
    xa = sdma("xa", T.X[:, 0:2048], T.x[:, 0:2048])
    xb = sdma("xb", T.X[:, 2048:H], T.x[:, 2048:H])

    v_eq = vec(lambda: V.memset(T.EQ[:, :, :], 1.0))
    v_bm = vec(lambda: V.memset(T.BM[:, :], 1.0))
    v_nw = vec(lambda: V.memset(T.NW[:, 0:H], 0.0))
    GE, IE = AluOpType.is_ge, AluOpType.is_equal
    g_eq = gps(lambda: g.affine_select(T.EQ[:, :, :], T.EQ[:, :, :], [[1, 16], [-1, 16]], IE, 0.0, 0, 0), v_eq)
    g_b1 = gps(lambda: g.affine_select(T.BM[:, :], T.BM[:, :], [[-2, 2], [-16, 8]], GE, 0.0, 0, 1), v_bm)
    g_bm = gps(lambda: g.affine_select(T.BM[:, :], T.BM[:, :], [[2, 2], [16, 8]], GE, 0.0, 1, -1), g_b1)
    g_li = gps(lambda: g.iota(T.LI[:, 0:1], [[0, 1]], 0, 1))

    def iot(ap, pat, b):
        return gps(lambda: g.iota(ap, pat, b, 0, allow_small_or_imprecise_dtypes=True))
    iot(T.HI[:, :], [[256, 2], [0, 4]], base + H)
    iot(T.OF[:, :], [[0, 2], [64, 4]], 0)
    g_si = iot(T.SI[:, :], [[1, 64]], 0)
    g_n3 = iot(T.N3[:, 0:2048], [[0, 2048]], 0)

    def split(a, h, l, ld):
        t = vec(lambda: V.tensor_copy(h[:, :], a[:, :]), ld)
        return vec(lambda: V.tensor_tensor(l[:, :], a[:, :], h[:, :], SUB), t)
    v_nl = split(T.NA, T.NH, T.NL, ldn)
    v_pl = split(T.PA, T.PH, T.PL, ldp)
    v_tl = split(T.TA, T.TH, T.TL, ldt)
    v_fw = vec(lambda: V.tensor_copy(T.FW[:, 0:28], T.FA[:, :]), ldf)
    v_la = vec(lambda: V.tensor_scalar(T.LA[:, 0:1], T.LI[:, 0:1], 15, None, AluOpType.bitwise_and), g_li)
    v_l2 = vec(lambda: V.tensor_scalar(T.LM[:, 0:1], T.LA[:, 0:1], 2.0, None, IE), v_la)
    v_l3 = vec(lambda: V.tensor_scalar(T.LM[:, 4:5], T.LA[:, 0:1], 3.0, None, IE), v_la)
    v_h = vec(lambda: V.tensor_scalar(T.HI[:, :], T.HI[:, :], T.LM[:, 0:1], None, MUL), v_l2, g_si)
    v_o = vec(lambda: V.tensor_scalar(T.OF[:, :], T.OF[:, :], T.LM[:, 4:5], None, MUL), v_l3, g_si)
    v_bb = vec(lambda: V.tensor_tensor(T.BB[:, :], T.HI[:, :], T.OF[:, :], ADD), v_h, v_o)
    v_n3 = vec(lambda: V.memset(T.N3[:, 2048:H], 0.0))
    v_x0 = vec(lambda: V.tensor_scalar(T.NX[:, 0:1024:4], T.NA[:, :], 4.0, None, MUL), ldn)
    v_x3 = vec(lambda: V.tensor_scalar(T.NX[:, 3:1024:4], T.PA[:, :], 4.0, 1.0, MUL, ADD), ldp)

    sdma("lan1", lane(T.NW, 0), T.NH[:, :], v_nw, v_nl)
    sdma("lan1", lane(T.NW, 1), T.NL[:, :])
    for k in (2, 4):
        sdma("lan1", lane(T.NW, k), T.PH[:, :], v_pl)
        sdma("lan1", lane(T.NW, k + 1), T.PL[:, :])
    sdma("lan1", lane(T.NW, 6), T.TH[:, :], v_tl)
    lan1 = sdma("lan1", lane(T.NW, 7), T.TL[:, :])
    sdma("lan3", lane(T.N3, 2), T.TH[:, :], v_n3, g_n3)
    lan3 = sdma("lan3", lane(T.N3, 3), T.TL[:, :])
    xc = sdma("xc", T.X2[:, 0:2048], T.x[:, 0:2048])
    xd = sdma("xd", T.X2[:, 2048:H], T.x[:, 2048:H])

    def build(u):
        tok = None
        d = T["D%d" % u]
        for k in range(8):
            tok = act(lambda: S.activation(d[:, :, 16 * k:16 * k + 16], T.EQ[:, :, :], IDN,
                                           scale=T.BM[:, 8 * u + k:8 * u + k + 1]), g_eq, g_bm)
        return tok
    s_d0 = build(0)
    s_d1 = build(1)
    s_xf = act(lambda: S.activation(T.XF[:, :], T.X[:, :].indirect(T.FW[:, 0:28]), IDN), v_fw, xa, xb)
    s_c3 = None
    for i in range(NS):
        s_c3 = act(lambda: S.activation(T.C3[:, E * i:E * i + E], T.SI[:, :], IDN, bias=T.BB[:, i:i + 1],
                                        scale=T.LM[:, 4:5]), v_bb, g_si)
    s_ce = act(lambda: S.activation(T.NW[:, H:HX], T.C3[:, :], IDN), s_c3)

    v_r1 = vec(lambda: V.tensor_copy(T.R1[:, :], T.NW[:, 0:H].indirect(T.FW[:, 0:28])), lan1, v_fw)
    t_nq = [wrap(0, 64, T.D0, T.NW, 0, lan1, s_d0)]
    t_nf = wrap(1, 28, T.D0, T.R1, 0, v_r1)
    t_nq += [wrap(3, 64, T.D0, T.NW, 64), wrap(4, 64, T.D0, T.NW, 128)]
    t_pf = wrap(2, 28, T.D1, T.R1, 0, s_d1)
    t_nq.append(wrap(5, 64, T.D0, T.NW, 192))
    v_nq = [evac(qd(T.NXW, 0), 0, 64, t_nq[0])]
    v_nf = evac(T.NFW[:, 0:28], 1, 28, t_nf)
    v_mf = vec(lambda: V.tensor_tensor(T.MF[:, :], T.X[:, :].indirect(T.NFW[:, 0:28]), T.XF[:, :], ADD), v_nf, s_xf, xa, xb)
    v_nq.append(evac(qd(T.NXW, 1), 3, 64, t_nq[1]))
    v_c3 = vec(lambda: V.tensor_copy(T.N3[:, :].indirect(T.FW[:, 0:28]), T.C3[:, :]), lan3, s_c3)
    v_nq.append(evac(qd(T.NXW, 2), 4, 64, t_nq[2]))
    v_pf = evac(T.PFW[:, 0:28], 2, 28, t_pf)
    v_ee = vec(lambda: V.tensor_copy(T.EE[:, :], T.N3[:, :].indirect(T.PFW[:, 0:28])), v_pf, v_c3)
    v_nq.append(evac(qd(T.NXW, 3), 5, 64, t_nq[3]))
    t_tw = [wrap(6, 64, T.D1, T.N3, 0, v_c3), wrap(7, 64, T.D1, T.N3, 64)]
    t_e = wrap(1, 28, T.D1, T.EE, 0, v_ee, v_nf)
    t_tw.append(wrap(0, 64, T.D1, T.N3, 128, v_nq[0]))
    t_tw.append(wrap(2, 64, T.D1, T.N3, 192, v_pf))

    def order():
        used, plan = [], []
        away = [q for q in range(8) if q != r and topo.chip(cores[q]) != topo.chip(core)]
        near = [q for q in range(8) if q != r and topo.chip(cores[q]) == topo.chip(core)]
        for q in away + near:
            es = topo.engines(core, cores[q])
            es = es[::2] + es[1::2]
            e = [k for k in es if k not in used][0]
            used.append(e)
            plan.append((q, e))
        return plan
    plan = order()

    def send(src, dst, d0, rs, ls, *toks):
        wait("g", g, toks)
        tr = []
        for q, e in plan:
            rid, pid, _se = topo.addr(cores[q])
            i, k = slot(r, q), slot(q, r)
            tr.append(RemoteDMATransfer(dst_ids=[DstId(rid=rid, pnc=pid)], dma_engine_mask=1 << e, remote_sem=T.sem[rs],
                                        src=src[:, E * i:E * i + E], dst=dst[:, d0 + E * k:d0 + E * k + E]))
        g.remote_dma_fused(tr, local_sem=T.sem[ls])
        total[ls] = NS
        total[rs] = NS
    a1, an, a2 = ("a1", NS), ("an", NS), ("a2", NS)
    send(T.R1, T.RN, 0, "an", "sn", v_r1)
    send(T.MF, T.MX, H, "a1", "s1", v_mf)
    sdma("rnl", T.NW[4:128:16, H:HX], T.RN[4:128:16, :], an, s_ce)
    rnl = sdma("rnl", T.NW[5:128:16, H:HX], T.RN[5:128:16, :])

    def m_pass(k):
        return vec(lambda: V.tensor_tensor(rows(T.MX, k), T.X[:, :].indirect(qd(T.NXW, k)), rows(T.X2, k), ADD),
                   v_nq[k], xa, xb, xc if k < 2 else xd)
    v_m = [m_pass(0)]
    v_tw = [evac(qd(T.TWL, 0), 6, 64, t_tw[0])]
    v_m.append(m_pass(1))
    m2a = sdma("m2a", T.M2[:, 0:2048], T.MX[:, 0:2048], v_m[1])
    v_tw.append(evac(qd(T.TWL, 1), 7, 64, t_tw[1]))
    v_m.append(m_pass(2))
    v_e = evac(T.EW[:, 0:28], 1, 28, t_e)
    v_tw.append(evac(qd(T.TWL, 2), 0, 64, t_tw[2]))
    v_m.append(m_pass(3))
    v_tw.append(evac(qd(T.TWL, 3), 2, 64, t_tw[3]))
    m2b = sdma("m2b", T.M2[:, 2048:H], T.MX[:, 2048:H], v_m[3])

    s_nn = None
    for k in range(4):
        s_nn = act(lambda: S.activation(rows(T.NN, k), T.NW[:, 0:H].indirect(qd(T.NXW, k)), IDN), lan1, v_nq[k])

    def q_pass(h):
        return vec(lambda: V.tensor_tensor(T.Q[:, 2048 * h:2048 * h + 2048], T.MX[:, 0:H].indirect(T.NXW[:, 128 * h:128 * h + 128]),
                                           T.M2[:, 2048 * h:2048 * h + 2048], ADD), v_m[3], v_nq[3], (m2a, m2b)[h])
    v_vv = vec(lambda: V.tensor_copy(T.VV[:, :], T.MX[:, :].indirect(T.EW[:, 0:28])), a1, v_m[3], v_e)
    send(T.VV, T.UX, H, "a2", "s2", v_vv)
    v_qa = q_pass(0)
    v_qb = q_pass(1)

    s_nt, t_pt = [], []
    free = [v_nq[1], v_nq[2], v_nq[3], v_tw[0]]
    for k in range(4):
        s_nt.append(act(lambda: S.activation(rows(T.NT, k), T.NW[:, :].indirect(qd(T.TWL, k)), IDN), rnl, s_ce, v_tw[k]))
        t_pt.append(wrap(3 + k, 64, T.D1, T.NT, 64 * k, s_nt[k], free[k]))

    sdma("otn", T.TNH[:, :], lane(T.NN, 6), s_nn)
    otn = sdma("otn", T.TNL[:, :], lane(T.NN, 7))
    sdma("opt", T.PTH[:, :], lane(T.NT, 4), s_nt[3])
    opt = sdma("opt", T.PTL[:, :], lane(T.NT, 5))

    u, u2 = [], []
    for k in range(4):
        u.append(act(lambda: S.activation(rows(T.UX, k), T.MX[:, :].indirect(qd(T.TWL, k)), IDN), a1, v_m[3], v_tw[k]))
        u2.append(sdma("u2%d" % k, rows(T.U2, k), rows(T.UX, k), u[k]))

    v_t1 = vec(lambda: V.tensor_tensor(T.TMP[:, :], T.TNH[:, :], T.TNL[:, :], ADD), otn)
    v_x1 = vec(lambda: V.tensor_scalar(T.NX[:, 1:1024:4], T.TMP[:, :], 4.0, 3.0, MUL, ADD), v_t1)
    v_pt = [evac(qd(T.PTW, k), 3 + k, 64, t_pt[k]) for k in range(4)]
    v_t2 = vec(lambda: V.tensor_tensor(T.TMP2[:, :], T.PTH[:, :], T.PTL[:, :], ADD), opt)
    v_x2 = vec(lambda: V.tensor_scalar(T.NX[:, 2:1024:4], T.TMP2[:, :], 4.0, 2.0, MUL, ADD), v_t2)
    sdma("stn", T.nx[:, :], T.NX[:, :], v_x0, v_x1, v_x2, v_x3)

    for a, b in CHUNKS:
        s_ye = act(lambda: S.activation(T.Y[:, 32 * a:32 * b:2], T.Q[:, :].indirect(T.NXW[:, a:b]), IDN), v_qa, v_qb)
        v_yo = vec(lambda: V.tensor_tensor(T.Y[:, 32 * a + 1:32 * b:2], T.UX[:, :].indirect(T.PTW[:, a:b]), T.U2[:, 16 * a:16 * b],
                                           ADD), a2, u2[a // 64], v_pt[a // 64], *u)
        sdma("sty", T.y[:, 32 * a:32 * b], T.Y[:, 32 * a:32 * b], s_ye, v_yo)

    wait("g", g, [(s, total[s]) for s in total])
